import numpy as np
import ml_dtypes


def mxq(x, axis, fmt="e4m3"):
    dtype, down = {"e4m3": (ml_dtypes.float8_e4m3fn, 7), "e5m2": (ml_dtypes.float8_e5m2, 14)}[fmt]
    v = np.moveaxis(np.asarray(x, np.float32).astype(ml_dtypes.bfloat16).astype(np.float64), axis, -1)
    blocks = v.reshape(v.shape[:-1] + (-1, 32))
    amax = np.abs(blocks).max(-1, keepdims=True)
    byte = np.maximum(np.where(amax > 0, np.frexp(amax)[1] - 1 + 127, 0) - down, 1)
    scale = np.exp2(byte - 127.0)
    codes = (blocks / scale).astype(np.float32).astype(dtype).astype(np.float64)
    return np.moveaxis((codes * scale).reshape(v.shape), -1, axis)


WIDE = False


def mx_kscale(k):
    if not WIDE:
        return np.ones(k)
    levels = np.array([10, -10, 5, -5, 0])
    if k % 512:
        return np.exp2(np.random.permutation(np.resize(levels, k // 32))).repeat(32)
    a = np.empty((k // 512, 16))
    for p in range(k // 512):
        a[p, :8] = np.random.permutation(np.resize(levels, 8))
        for g in range(8):
            far = levels[np.abs(levels - a[p, g]) >= 10]
            a[p, g + 8] = far[np.random.randint(len(far))]
    return np.exp2(a.ravel()).repeat(32)


def f64(x):
    return np.asarray(x).astype(np.float64)


def striped(idx):
    return np.tile(idx.reshape(-1, 16).T, (8, 1)).astype(np.uint16)


def unstriped(offs):
    return offs[:16].T.reshape(-1).astype(np.int64)


E2M1 = np.array([0.0, 0.5, 1.0, 1.5, 2.0, 3.0, 4.0, 6.0, -0.0, -0.5, -1.0, -1.5, -2.0, -3.0, -4.0, -6.0])


def pack_weight(w, fmt):
    k, n = w.shape
    w = f64(np.asarray(w, np.float32).astype(ml_dtypes.bfloat16)).reshape(k // 32, 32, n)
    amax = np.abs(w).max(1)
    if fmt == "e4m3":
        byte = np.frexp(amax)[1] - 1 + 127 - 7
    else:
        mant, ex = np.frexp(amax / 6.0)
        byte = np.where(mant > 0.5, ex, ex - 1) + 127
    byte = np.clip(np.where(amax > 0, byte, 1), 1, 254)
    scaled = (w * np.exp2(127.0 - byte)[:, None, :]).reshape(k, n).astype(np.float32)
    by_word = np.ascontiguousarray(scaled.reshape(k // 512, 128, 4, n).transpose(0, 1, 3, 2))
    if fmt == "e4m3":
        words = by_word.astype(ml_dtypes.float8_e4m3fn).view(np.uint8)
    else:
        c = by_word.astype(ml_dtypes.float4_e2m1fn).view(np.uint8) & 0xF
        words = (c[..., 0::2] | (c[..., 1::2] << 4)).reshape(k // 512, 128, 2 * n)
    return np.ascontiguousarray(words), np.ascontiguousarray(byte.astype(np.uint8).reshape(k // 512, 16, n))


def unpack_weight(words, scales, fmt):
    g, _, n = scales.shape
    words = np.ascontiguousarray(words).reshape(g, 128, n, -1)
    if fmt == "e4m3":
        vals = words.view(ml_dtypes.float8_e4m3fn).astype(np.float64)
    else:
        nib = np.empty((g, 128, n, 4), np.uint8)
        nib[..., 0::2] = words & 0xF
        nib[..., 1::2] = words >> 4
        vals = E2M1[nib]
    vals = vals * np.repeat(np.exp2(scales.astype(np.float64) - 127.0), 8, axis=1)[..., None]
    return vals.transpose(0, 1, 3, 2).reshape(g * 512, n)


def gelu(v):
    return 0.5 * v * (1.0 + np.tanh(np.sqrt(2.0 / np.pi) * (v + 0.044715 * v**3)))


def bf(x):
    return np.asarray(x, np.float32).astype(ml_dtypes.bfloat16)


def planes(Y):
    n, m = Y.shape
    b = f64(bf(Y)).reshape(n // 32, 32, m)
    amax = np.abs(b).max(1)
    byte = np.clip(np.where(amax > 0, np.frexp(amax)[1] - 1 + 127 - 7, 1), 1, 254)
    codes = (b * np.exp2(127.0 - byte)[:, None, :]).reshape(n, m).astype(np.float32).astype(ml_dtypes.float8_e4m3fn).view(np.uint8)
    words = codes.reshape(n // 512, 128, 4, m).transpose(0, 1, 3, 2)
    return np.ascontiguousarray(words), np.ascontiguousarray(byte.astype(np.uint8).reshape(n // 512, 16, m))


K, K2, T, S, H, N, T2 = 1024, 1536, 2048, 512, 1024, 512, 1024

def setup_inputs():
    n = np.random.standard_normal
    s = mx_kscale(K)[:, None]
    s2 = mx_kscale(K2)[:, None]
    u = mx_kscale(H)[:, None]
    tab_words, tab_scales = pack_weight(n((K, T)) * s, "e4m3")
    tab2_words, tab2_scales = pack_weight(n((K2, T)) * s2, "e4m3")
    w1_words, w1_scales = pack_weight(1.3 * n((K, H)) / np.sqrt(K) / s, "e2m1")
    w3_words, w3_scales = pack_weight(1.2 * n((H, N)) * np.exp(0.8 * n(N)) / np.sqrt(H) / u, "e4m3")
    return {
        "tab_words": tab_words, "tab_scales": tab_scales,
        "tab2_words": tab2_words, "tab2_scales": tab2_scales,
        "offs": striped(np.random.permutation(T)[:S]),
        "offs2": striped(np.random.permutation(T)[:S]),
        "offs3": striped(np.random.permutation(T2)[:S]),
        "offs4": striped(np.random.permutation(T2)[:S]),
        "w1_words": w1_words, "w1_scales": w1_scales,
        "w2": (0.56 * n((K2, H)) / np.sqrt(K2) / s2).astype(np.float32),
        "w3_words": w3_words, "w3_scales": w3_scales,
        "wg1": np.exp(0.3 * n((128, S))).astype(np.float32),
        "wg2": np.exp(0.3 * n((128, S))).astype(np.float32),
        "chart": (0.6 * n((H, T2))).astype(np.float32),
        "gz": (np.exp(0.3 * n(H)) * u[:, 0]).astype(np.float32),
    }

def reference(tab_words, tab_scales, tab2_words, tab2_scales, offs, offs2, offs3, offs4, w1_words, w1_scales, w2, w3_words, w3_scales, wg1, wg2, chart, gz):
    v = unpack_weight(tab_words, tab_scales, "e4m3")[:, unstriped(offs)]
    v2 = unpack_weight(tab2_words, tab2_scales, "e4m3")[:, unstriped(offs2)]
    h1 = np.tanh(unpack_weight(w1_words, w1_scales, "e2m1").T @ v)
    d = mxq(f64(w2), 0, "e4m3").T @ v2
    h2 = d * np.cos(d)
    pa = np.zeros((H, T2))
    pa[:, unstriped(offs3)] = np.tile(f64(wg1), (H // 128, 1)) * h1
    pb = np.zeros((H, T2))
    pb[:, unstriped(offs4)] = np.tile(f64(wg2), (H // 128, 1)) * h2
    z = (np.maximum(pa, f64(chart)) - pb) * f64(gz)[:, None]
    e = unpack_weight(w3_words, w3_scales, "e4m3").T @ mxq(z, 0, "e4m3")
    y = 0.5 * e * (1.0 + np.tanh(0.7978845608028654 * (e + 0.044715 * e ** 3)))
    words, scales = planes(y)
    return y, words, scales

@@ -1,0 +1,374 @@
+import math
+from contextlib import ExitStack
+
+import concourse.mybir as mybir
+from concourse.masks import make_identity
+
+K, K2, T, S, H, N, T2 = 1024, 1536, 2048, 512, 1024, 512, 1024
+FLOPS = 2 * (K * H * S + K2 * H * S + H * N * T2)
+
+F32 = mybir.dt.float32
+BF16 = mybir.dt.bfloat16
+I32 = mybir.dt.int32
+U32 = mybir.dt.uint32
+U16 = mybir.dt.uint16
+U8 = mybir.dt.uint8
+FP8X4 = mybir.dt.float8_e4m3fn_x4
+FP4X4 = mybir.dt.float4_e2m1fn_x4
+ACT = mybir.ActivationFunctionType
+ALU = mybir.AluOpType
+
+P = 128
+PACK = 4
+K_PASS = P * PACK
+SLICES = H // P
+GROUPS = H // K_PASS
+SL_PER_GROUP = K_PASS // P
+QUADS = 4
+PA_PAGES = 4
+PB_PAGES = 2
+HALF = 512
+CH = 256
+
+
+def tile_list_seabed_mosaic_scores_kernel(
+    tc, tab_words, tab_scales, tab2_words, tab2_scales, offs, offs2, offs3, offs4,
+    w1_words, w1_scales, w2, w3_words, w3_scales, wg1, wg2, chart, gz, out_0, out_1, out_2,
+):
+    nc = tc.nc
+    with ExitStack() as ctx:
+        lists = ctx.enter_context(tc.tile_pool(name="lists", bufs=1))
+        sb = ctx.enter_context(tc.tile_pool(name="sb", bufs=1))
+        ps = ctx.enter_context(tc.psum_pool(name="ps", bufs=1))
+
+        def keep(name, shape, dtype):
+            return sb.tile(shape, dtype, name=name, tag=name, bufs=1, align_bytes=64)
+
+        def ring(tag, bufs, shape, dtype):
+            return sb.tile(shape, dtype, name=tag, tag=tag, bufs=bufs, align_bytes=64)
+
+        def bank(tag, bufs, shape):
+            return ps.tile(shape, F32, name=tag, tag=tag, bufs=bufs)
+
+        def quad_rows(q, rows):
+            return slice(32 * q, 32 * q + rows)
+
+        tab_sc = keep("tab_sc", [P, 2, T], U8)
+        w1_sc = keep("w1_sc", [P, 2, H], U8)
+        tab2_sc = keep("tab2_sc", [P, T], U8)
+        w3_sc = keep("w3_sc", [P, N], U8)
+        gz_rows = keep("gz_rows", [P, P], F32)
+        nc.vector.memset(tab_sc[:, 0, :].bitcast(I32), 0)
+        nc.gpsimd.memset(tab_sc[:, 1, :].bitcast(I32), 0)
+        nc.vector.memset(w1_sc[:].bitcast(I32), 0)
+        nc.vector.memset(tab2_sc[:].bitcast(I32), 0)
+        pa = [keep("pa%d" % i, [P, T2], F32) for i in range(PA_PAGES)]
+        pb = [keep("pb%d" % i, [P, T2], F32) for i in range(PB_PAGES)]
+        ident = keep("ident", [P, P], F32)
+        for page in pa:
+            nc.gpsimd.memset(page[:], 0.0)
+        nc.gpsimd.memset(gz_rows[:], 0.0)
+        make_identity(nc, ident[:])
+        nc.gpsimd.memset(w3_sc[:].bitcast(I32), 0)
+        for page in pb:
+            nc.gpsimd.memset(page[:], 0.0)
+
+        def load_list(name, src):
+            tile = lists.tile([P, S // 16], U16, name=name, tag=name)
+            nc.sync.dma_start(tile[:], src)
+            return tile
+
+        def load_table(tag, words, a, parts=1):
+            tile = ring(tag, words.shape[0], [P, T], I32)
+            src = words[a].rearrange("p t i -> p (t i)").bitcast(I32)
+            for c in range(0, T, T // parts):
+                nc.sync.dma_start(out=tile[:, c : c + T // parts], in_=src[:, c : c + T // parts])
+            return tile
+
+        idx1 = load_list("idx1", offs)
+        idx3 = load_list("idx3", offs3)
+        idx2 = load_list("idx2", offs2)
+        idx4 = load_list("idx4", offs4)
+        tab_w = [load_table("tab_w", tab_words, 0, 4)]
+        for q in range(QUADS):
+            nc.sync.dma_start(
+                out=tab_sc[quad_rows(q, 4), :, :].bitcast(I32),
+                in_=tab_scales[:, 4 * q : 4 * q + 4, :].rearrange("a q t -> q a t").bitcast(I32),
+            )
+        tab_w.append(load_table("tab_w", tab_words, 1))
+        w1_w = keep("w1_w", [P, 2, 2 * H], U8)
+        nc.sync.dma_start(out=w1_w[:].bitcast(I32), in_=w1_words.rearrange("a p c -> p a c").bitcast(I32))
+        for q in range(QUADS):
+            nc.sync.dma_start(
+                out=w1_sc[quad_rows(q, 4), :, :].bitcast(I32),
+                in_=w1_scales[:, 4 * q : 4 * q + 4, :].rearrange("a q c -> q a c").bitcast(I32),
+            )
+        wg1_sb = keep("wg1_sb", [P, S], F32)
+        nc.sync.dma_start(out=wg1_sb[:], in_=wg1)
+
+        whole_list = [(slice(0, S), slice(0, S // 16))]
+        list_halves = [(slice(c, c + S // 2), slice(c // 16, (c + S // 2) // 16)) for c in (0, S // 2)]
+        v_sc = keep("v_sc", [P, 2, S], U8)
+        v_w = keep("v_w", [P, 2, S], U32)
+        for a in range(2):
+            nc.vector.tensor_copy(v_sc[:, a, :], tab_sc[:, a, :].indirect(idx1[:]))
+        nc.vector.tensor_copy(v_w[:, 0, :], tab_w[0][:].bitcast(U32).indirect(idx1[:]))
+        for cols, offsets in list_halves:
+            nc.vector.tensor_copy(v_w[:, 1, cols], tab_w[1][:].bitcast(U32).indirect(idx1[:, offsets]))
+
+        h1 = []
+        for s in range(SLICES):
+            tile = ring("h1", SLICES, [P, S], F32)
+            for cols, offsets in list_halves if s == 0 else whole_list:
+                acc = bank("mm", 3, [P, cols.stop - cols.start])
+                for a in range(2):
+                    nc.tensor.matmul_mx(
+                        out=acc[:],
+                        lhsT=w1_w[:, a, 2 * P * s : 2 * P * (s + 1)].bitcast(FP4X4),
+                        lhsT_scale=w1_sc[:, a, P * s : P * (s + 1)],
+                        rhs=v_w[:, a, cols].bitcast(FP8X4),
+                        rhs_scale=v_sc[:, a, cols],
+                        start=(a == 0), stop=(a == 1),
+                    )
+                nc.scalar.activation(tile[:, cols], acc[:], ACT.Tanh)
+            h1.append(tile)
+
+        def place_a(s):
+            for cols, offsets in list_halves if s == 0 else whole_list:
+                nc.vector.tensor_tensor(
+                    pa[s % PA_PAGES][:].indirect(idx3[:, offsets]), h1[s][:, cols], wg1_sb[:, cols], ALU.mult
+                )
+
+        for s in range(PA_PAGES):
+            place_a(s)
+
+        for q in range(QUADS):
+            nc.sync.dma_start(
+                out=tab2_sc[quad_rows(q, 12), :].bitcast(I32),
+                in_=tab2_scales[:, 4 * q : 4 * q + 4, :].bitcast(I32),
+            )
+        tab2_w = [load_table("tab2_w", tab2_words, a) for a in range(3)]
+        v2_sc = keep("v2_sc", [P, S], U8)
+        v2_w = keep("v2_w", [P, 3, S], U32)
+        nc.vector.tensor_copy(v2_sc[:], tab2_sc[:].indirect(idx2[:]))
+        for a in range(3):
+            nc.vector.tensor_copy(v2_w[:, a, :], tab2_w[a][:].bitcast(U32).indirect(idx2[:]))
+
+        nc.sync.dma_start(out=gz_rows[0:SLICES, :], in_=gz.rearrange("(s p) -> s p", p=P))
+        gz_ps = bank("tw", 2, [P, P])
+        nc.tensor.transpose(gz_ps[:], gz_rows[:], ident[:])
+        gz_col = keep("gz_col", [P, SLICES], F32)
+        nc.scalar.copy(gz_col[:], gz_ps[:, 0:SLICES])
+        wg2_sb = ring("wg2_w3", 1, [P, S], F32)
+        nc.sync.dma_start(out=wg2_sb[:], in_=wg2)
+
+        w2_w = keep("w2_w", [P, 3, H], U32)
+        w2_sc = keep("w2_sc", [P, 3, H], U8)
+
+        def load_w2(h, a):
+            raw = ring("stage", 3, [P, PACK, HALF], F32)
+            nc.sync.dma_start(
+                out=raw[:],
+                in_=w2[K_PASS * a : K_PASS * (a + 1), HALF * h : HALF * (h + 1)].rearrange("(p i) c -> p i c", i=PACK),
+            )
+            return raw
+
+        def quantise_w2(h, a, raw):
+            cols = slice(HALF * h, HALF * (h + 1))
+            grouped = ring("w2_bf", 3, [P, HALF, PACK], BF16)
+            nc.scalar.copy(
+                grouped[:].rearrange("p (c n) i -> p c i n", n=4),
+                raw[:].rearrange("p i (c n) -> p c i n", n=4),
+            )
+            nc.vector.quantize_mx(
+                out=w2_w[:, a, cols].bitcast(FP8X4),
+                scales=w2_sc[:, a, cols],
+                in_=grouped[:].rearrange("p c i -> p (c i)"),
+            )
+
+        def load_chart(tag, bufs, pair):
+            tile = ring(tag, bufs, [P, 2, T2], F32)
+            nc.sync.dma_start(
+                out=tile[:], in_=chart[2 * P * pair : 2 * P * (pair + 1), :].rearrange("(s p) j -> p s j", p=P)
+            )
+            return tile
+
+        for h in range(2):
+            for a in range(3):
+                quantise_w2(h, a, load_w2(h, a))
+        chart_sb = [load_chart("tab_w", 2, 0), load_chart("tab_w", 2, 1)]
+        chart_sb.extend([load_chart("tab2_w", 3, 2), load_chart("tab2_w", 3, 3)])
+
+        w3_raw = keep("w3_raw", [P, GROUPS, N], I32)
+        nc.sync.dma_start(out=w3_raw[:], in_=w3_words.rearrange("a p c i -> p a (c i)").bitcast(I32))
+        for q in range(QUADS):
+            nc.sync.dma_start(
+                out=w3_sc[quad_rows(q, 8), :].bitcast(I32),
+                in_=w3_scales[:, 4 * q : 4 * q + 4, :].bitcast(I32),
+            )
+        w3_sd = keep("w3_sd", [P, PACK, P], U8)
+
+        def deal_w3():
+            w3_w = ring("wg2_w3", 1, [P, GROUPS, PACK, P], I32)
+            nc.vector.tensor_copy(w3_w[:], w3_raw[:].rearrange("p a (q t) -> p a t q", t=PACK))
+            nc.vector.tensor_copy(w3_sd[:], w3_sc[:].rearrange("p (q t) -> p t q", t=PACK))
+            return w3_w
+
+        def reduce_d(s):
+            acc = bank("mm", 3, [P, S])
+            for a in range(3):
+                nc.tensor.matmul_mx(
+                    out=acc[:],
+                    lhsT=w2_w[:, a, P * s : P * (s + 1)].bitcast(FP8X4),
+                    lhsT_scale=w2_sc[:, a, P * s : P * (s + 1)],
+                    rhs=v2_w[:, a, :].bitcast(FP8X4),
+                    rhs_scale=v2_sc[4 * a : P, :],
+                    start=(a == 0), stop=(a == 2),
+                )
+            turns = ring("turns", 4, [P, S], F32) if s < SLICES - 1 else ring("last", 1, [P, S], F32)
+            nc.scalar.activation(turns[:], acc[:], ACT.Abs, scale=1.0 / (2.0 * math.pi))
+            whole = ring("whole", 2, [P, S], U32)
+            nc.scalar.activation(whole[:], turns[:], ACT.Relu, bias=-0.25)
+            nc.vector.scalar_tensor_tensor(
+                out=turns[:], in0=turns[:], scalar=0.25, in1=whole[:].bitcast(I32), op0=ALU.subtract, op1=ALU.subtract
+            )
+            return acc, turns
+
+        z_t = {}
+
+        d_acc = {}
+        phase = {}
+        upper = {}
+
+        def cosine(s):
+            nc.scalar.activation(phase[s][:], phase[s][:], ACT.Sin, scale=2.0 * math.pi)
+
+        def take_max(s):
+            upper[s] = chart_sb[s // 2][:, s % 2, :]
+            nc.vector.tensor_tensor(upper[s], pa[s % PA_PAGES][:], upper[s], ALU.max)
+            if s + PA_PAGES < SLICES:
+                place_a(s + PA_PAGES)
+
+        def gain_max(s):
+            nc.scalar.activation(upper[s], upper[s], ACT.Copy, scale=gz_col[:, s : s + 1])
+
+        def place_b(s):
+            nc.vector.scalar_tensor_tensor(
+                out=phase[s][:], in0=d_acc[s][:], scalar=gz_col[:, s : s + 1], in1=phase[s][:],
+                op0=ALU.mult, op1=ALU.mult,
+            )
+            nc.vector.tensor_tensor(pb[s % PB_PAGES][:].indirect(idx4[:]), phase[s][:], wg2_sb[:], ALU.mult)
+
+        def turn_sum(s):
+            g, sl = divmod(s, SL_PER_GROUP)
+            for h in range(T2 // HALF):
+                if sl == 0:
+                    z_t[g, h] = ring("z_t", 3, [P, 4, 2, P, 2], BF16)
+                tsum = bank("tsum", 3, [P, 4, P])
+                for term, src in enumerate((upper[s], pb[s % PB_PAGES])):
+                    for b in range(4):
+                        cols = slice(HALF * h + P * b, HALF * h + P * (b + 1))
+                        nc.tensor.matmul(
+                            tsum[:, b, :], src[:, cols], ident[:],
+                            start=(term == 0 and b == 0), stop=(term == 1 and b == 3), is_transpose=True,
+                        )
+                nc.scalar.copy(
+                    z_t[g, h][:, :, :, 32 * sl : 32 * (sl + 1), :],
+                    tsum[:].rearrange("j b (q u e) -> j b u q e", u=2, e=2),
+                )
+
+        z_w = {}
+        z_sc = keep("z_sc", [P, GROUPS, T2], U8)
+        z_bf = {}
+
+        def group_z(g, c):
+            h, b0 = divmod(CH * c // P, 4)
+            words = z_t[g, h][:].rearrange("j b u p e -> j b u (p e)").bitcast(F32)
+            turned = bank("tw", 2, [P, 2, 2, P])
+            for b in range(2):
+                for u in range(2):
+                    nc.tensor.transpose(turned[:, b, u, :], words[:, b0 + b, u, :], ident[:])
+            z_bf[g, c] = ring("z_bf", 6, [P, CH, PACK], BF16)
+            move = nc.scalar.copy if g == 0 else nc.vector.tensor_copy
+            move(
+                z_bf[g, c][:].bitcast(F32).rearrange("p (b j) u -> p b j u", b=2),
+                turned[:].rearrange("p b u j -> p b j u"),
+            )
+
+        def quantise_z(g, c):
+            cols = slice(CH * c, CH * (c + 1))
+            nc.vector.quantize_mx(
+                out=z_w[g][:, cols].bitcast(FP8X4),
+                scales=z_sc[:, g, cols],
+                in_=z_bf[g, c][:].rearrange("p j i -> p (j i)"),
+            )
+
+        y_w = keep("y_w", [P, T2], U32)
+        y_sc = keep("y_sc", [P, T2], U8)
+        y_rows = out_0.rearrange("(p t) j -> p t j", t=PACK)
+        y_words = out_1[0].rearrange("p m t -> p (m t)").bitcast(I32)
+
+        def score(c):
+            cols = slice(CH * c, CH * (c + 1))
+            y = ring("stage", 3, [P, PACK, CH], F32)
+            for pair in range(2):
+                acc = bank("mm", 3, [P, 2, CH])
+                for i in range(2):
+                    t = 2 * pair + i
+                    for g in range(GROUPS):
+                        nc.tensor.matmul_mx(
+                            out=acc[:, i, :],
+                            lhsT=w3_w[:, g, t, :].bitcast(FP8X4),
+                            lhsT_scale=w3_sd[4 * g : P, t, :],
+                            rhs=z_w[g][:, cols].bitcast(FP8X4),
+                            rhs_scale=z_sc[:, g, cols],
+                            start=(g == 0), stop=(g == GROUPS - 1),
+                        )
+                nc.scalar.activation(y[:, 2 * pair : 2 * pair + 2, :], acc[:], ACT.Gelu_apprx_tanh)
+            nc.sync.dma_start(out=y_rows[:, :, cols], in_=y[:])
+            grouped = ring("y_bf", 2, [P, CH, PACK], BF16)
+            nc.vector.tensor_copy(
+                grouped[:].rearrange("p (c n) t -> p c t n", n=4),
+                y[:].rearrange("p t (c n) -> p c t n", n=4),
+            )
+            nc.vector.quantize_mx(
+                out=y_w[:, cols].bitcast(FP8X4),
+                scales=y_sc[:, cols],
+                in_=grouped[:].rearrange("p j t -> p (j t)"),
+            )
+            nc.sync.dma_start(out=y_words[:, cols], in_=y_w[:, cols].bitcast(I32))
+
+        chunks = T2 // CH
+        take_max(0)
+        gain_max(0)
+        for s in range(2):
+            d_acc[s], phase[s] = reduce_d(s)
+        cosine(0)
+        for s in range(SLICES):
+            place_b(s)
+            if s + 2 < SLICES:
+                d_acc[s + 2], phase[s + 2] = reduce_d(s + 2)
+            if s + 1 < SLICES:
+                cosine(s + 1)
+                take_max(s + 1)
+            turn_sum(s)
+            if s + 1 < SLICES:
+                gain_max(s + 1)
+            if SL_PER_GROUP - 1 <= s < SL_PER_GROUP + 1:
+                for c in range(2):
+                    group_z(0, 2 * (s - SL_PER_GROUP + 1) + c)
+        w3_w = deal_w3()
+        z_w[0] = ring("last", 1, [P, T2], U32)
+        z_w[1] = keep("z_w1", [P, T2], U32)
+        for c in range(chunks):
+            quantise_z(0, c)
+        for c in range(chunks + 1):
+            if c < chunks:
+                group_z(1, c)
+                quantise_z(1, c)
+            if c > 0:
+                score(c - 1)
+        for q in range(QUADS):
+            nc.sync.dma_start(
+                out=out_2[0, 4 * q : 4 * q + 4, :].bitcast(I32), in_=y_sc[quad_rows(q, 4), :].bitcast(I32)
+            )

@@ -29,6 +29,8 @@ PA_PAGES = 4
 PB_PAGES = 2
 HALF = 512
 CH = 256
+W1_FIRST = 2
+LEAD = 2
 
 
 def tile_list_seabed_mosaic_scores_kernel(
@@ -62,49 +64,56 @@ def tile_list_seabed_mosaic_scores_kernel(
         nc.gpsimd.memset(tab_sc[:, 1, :].bitcast(I32), 0)
         nc.vector.memset(w1_sc[:].bitcast(I32), 0)
         nc.vector.memset(tab2_sc[:].bitcast(I32), 0)
-        pa = [keep("pa%d" % i, [P, T2], F32) for i in range(PA_PAGES)]
-        pb = [keep("pb%d" % i, [P, T2], F32) for i in range(PB_PAGES)]
+        pa = [keep("pa%d" % i, [P, T2], F32) for i in range(PA_PAGES - 1)]
         ident = keep("ident", [P, P], F32)
         for page in pa:
-            nc.gpsimd.memset(page[:], 0.0)
+            nc.vector.memset(page[:].bitcast(I32), 0)
         nc.gpsimd.memset(gz_rows[:], 0.0)
         make_identity(nc, ident[:])
         nc.gpsimd.memset(w3_sc[:].bitcast(I32), 0)
-        for page in pb:
-            nc.gpsimd.memset(page[:], 0.0)
 
         def load_list(name, src):
             tile = lists.tile([P, S // 16], U16, name=name, tag=name)
             nc.sync.dma_start(tile[:], src)
             return tile
 
-        def load_table(tag, words, a, parts=1):
+        def load_words(tile, words, a, cols):
+            nc.sync.dma_start(out=tile[:, cols], in_=words[a].rearrange("p t i -> p (t i)").bitcast(I32)[:, cols])
+
+        def load_table(tag, words, a):
             tile = ring(tag, words.shape[0], [P, T], I32)
-            src = words[a].rearrange("p t i -> p (t i)").bitcast(I32)
-            for c in range(0, T, T // parts):
-                nc.sync.dma_start(out=tile[:, c : c + T // parts], in_=src[:, c : c + T // parts])
+            load_words(tile, words, a, slice(0, T))
             return tile
 
-        idx1 = load_list("idx1", offs)
-        idx3 = load_list("idx3", offs3)
-        idx2 = load_list("idx2", offs2)
-        idx4 = load_list("idx4", offs4)
-        tab_w = [load_table("tab_w", tab_words, 0, 4)]
+        tab_w = [ring("tab_w", 2, [P, T], I32)]
+        load_words(tab_w[0], tab_words, 0, slice(0, T // 2))
         for q in range(QUADS):
             nc.sync.dma_start(
                 out=tab_sc[quad_rows(q, 4), :, :].bitcast(I32),
                 in_=tab_scales[:, 4 * q : 4 * q + 4, :].rearrange("a q t -> q a t").bitcast(I32),
             )
+        idx1 = load_list("idx1", offs)
+        load_words(tab_w[0], tab_words, 0, slice(T // 2, T))
         tab_w.append(load_table("tab_w", tab_words, 1))
-        w1_w = keep("w1_w", [P, 2, 2 * H], U8)
-        nc.sync.dma_start(out=w1_w[:].bitcast(I32), in_=w1_words.rearrange("a p c -> p a c").bitcast(I32))
+        w1_w = ring("w1_w", 1, [P, 2, 2 * H], U8)
+
+        def load_w1(first, last):
+            cols = slice(2 * P * first, 2 * P * last)
+            nc.sync.dma_start(
+                out=w1_w[:, :, cols].bitcast(I32), in_=w1_words[:, :, cols].rearrange("a p c -> p a c").bitcast(I32)
+            )
+
+        load_w1(0, W1_FIRST)
         for q in range(QUADS):
             nc.sync.dma_start(
                 out=w1_sc[quad_rows(q, 4), :, :].bitcast(I32),
                 in_=w1_scales[:, 4 * q : 4 * q + 4, :].rearrange("a q c -> q a c").bitcast(I32),
             )
+        idx3 = load_list("idx3", offs3)
         wg1_sb = keep("wg1_sb", [P, S], F32)
         nc.sync.dma_start(out=wg1_sb[:], in_=wg1)
+        load_w1(W1_FIRST, SLICES)
+        idx2 = load_list("idx2", offs2)
 
         whole_list = [(slice(0, S), slice(0, S // 16))]
         list_halves = [(slice(c, c + S // 2), slice(c // 16, (c + S // 2) // 16)) for c in (0, S // 2)]
@@ -133,6 +142,12 @@ def tile_list_seabed_mosaic_scores_kernel(
                 nc.scalar.activation(tile[:, cols], acc[:], ACT.Tanh)
             h1.append(tile)
 
+        late_pages = [ring(tag, 1, [P, T2], F32) for tag in ("v_w", "w1_w", "w1_sc")]
+        for page in late_pages:
+            nc.gpsimd.memset(page[:].bitcast(I32), 0)
+        pa.append(late_pages[0])
+        pb = late_pages[1:]
+
         def place_a(s):
             for cols, offsets in list_halves if s == 0 else whole_list:
                 nc.vector.tensor_tensor(
@@ -159,6 +174,7 @@ def tile_list_seabed_mosaic_scores_kernel(
         nc.tensor.transpose(gz_ps[:], gz_rows[:], ident[:])
         gz_col = keep("gz_col", [P, SLICES], F32)
         nc.scalar.copy(gz_col[:], gz_ps[:, 0:SLICES])
+        idx4 = load_list("idx4", offs4)
         wg2_sb = ring("wg2_w3", 1, [P, S], F32)
         nc.sync.dma_start(out=wg2_sb[:], in_=wg2)
 
@@ -166,7 +182,7 @@ def tile_list_seabed_mosaic_scores_kernel(
         w2_sc = keep("w2_sc", [P, 3, H], U8)
 
         def load_w2(h, a):
-            raw = ring("stage", 3, [P, PACK, HALF], F32)
+            raw = ring("stage", 4, [P, PACK, HALF], F32)
             nc.sync.dma_start(
                 out=raw[:],
                 in_=w2[K_PASS * a : K_PASS * (a + 1), HALF * h : HALF * (h + 1)].rearrange("(p i) c -> p i c", i=PACK),
@@ -210,7 +226,10 @@ def tile_list_seabed_mosaic_scores_kernel(
 
         def deal_w3():
             w3_w = ring("wg2_w3", 1, [P, GROUPS, PACK, P], I32)
-            nc.vector.tensor_copy(w3_w[:], w3_raw[:].rearrange("p a (q t) -> p a t q", t=PACK))
+            nc.vector.tensor_copy(
+                w3_w[:].rearrange("p a t (q n) -> p a q t n", n=4),
+                w3_raw[:].rearrange("p a (q n t) -> p a q t n", n=4, t=PACK),
+            )
             nc.vector.tensor_copy(w3_sd[:], w3_sc[:].rearrange("p (q t) -> p t q", t=PACK))
             return w3_w
 
@@ -263,7 +282,7 @@ def tile_list_seabed_mosaic_scores_kernel(
             g, sl = divmod(s, SL_PER_GROUP)
             for h in range(T2 // HALF):
                 if sl == 0:
-                    z_t[g, h] = ring("z_t", 3, [P, 4, 2, P, 2], BF16)
+                    z_t[g, h] = ring("z_t", 4, [P, 4, 2, P, 2], BF16)
                 tsum = bank("tsum", 3, [P, 4, P])
                 for term, src in enumerate((upper[s], pb[s % PB_PAGES])):
                     for b in range(4):
@@ -310,7 +329,7 @@ def tile_list_seabed_mosaic_scores_kernel(
 
         def score(c):
             cols = slice(CH * c, CH * (c + 1))
-            y = ring("stage", 3, [P, PACK, CH], F32)
+            y = ring("stage", 4, [P, PACK, CH], F32)
             for pair in range(2):
                 acc = bank("mm", 3, [P, 2, CH])
                 for i in range(2):
@@ -339,8 +358,9 @@ def tile_list_seabed_mosaic_scores_kernel(
             nc.sync.dma_start(out=y_words[:, cols], in_=y_w[:, cols].bitcast(I32))
 
         chunks = T2 // CH
-        take_max(0)
-        gain_max(0)
+        for s in range(LEAD):
+            take_max(s)
+            gain_max(s)
         for s in range(2):
             d_acc[s], phase[s] = reduce_d(s)
         cosine(0)
@@ -350,13 +370,13 @@ def tile_list_seabed_mosaic_scores_kernel(
                 d_acc[s + 2], phase[s + 2] = reduce_d(s + 2)
             if s + 1 < SLICES:
                 cosine(s + 1)
-                take_max(s + 1)
+            if s + LEAD < SLICES:
+                take_max(s + LEAD)
             turn_sum(s)
-            if s + 1 < SLICES:
-                gain_max(s + 1)
-            if SL_PER_GROUP - 1 <= s < SL_PER_GROUP + 1:
-                for c in range(2):
-                    group_z(0, 2 * (s - SL_PER_GROUP + 1) + c)
+            if s + LEAD < SLICES:
+                gain_max(s + LEAD)
+            if 4 <= s < 4 + chunks:
+                group_z(0, s - 4)
         w3_w = deal_w3()
         z_w[0] = ring("last", 1, [P, T2], U32)
         z_w[1] = keep("z_w1", [P, T2], U32)

@@ -25,12 +25,12 @@ SLICES = H // P
 GROUPS = H // K_PASS
 SL_PER_GROUP = K_PASS // P
 QUADS = 4
-PA_PAGES = 4
+PA_PAGES = 5
 PB_PAGES = 2
 HALF = 512
 CH = 256
 W1_FIRST = 2
-LEAD = 2
+LEAD = 4
 
 
 def tile_list_seabed_mosaic_scores_kernel(
@@ -64,7 +64,7 @@ def tile_list_seabed_mosaic_scores_kernel(
         nc.gpsimd.memset(tab_sc[:, 1, :].bitcast(I32), 0)
         nc.vector.memset(w1_sc[:].bitcast(I32), 0)
         nc.vector.memset(tab2_sc[:].bitcast(I32), 0)
-        pa = [keep("pa%d" % i, [P, T2], F32) for i in range(PA_PAGES - 1)]
+        pa = [keep("pa%d" % i, [P, T2], F32) for i in range(PA_PAGES - 2)]
         ident = keep("ident", [P, P], F32)
         for page in pa:
             nc.vector.memset(page[:].bitcast(I32), 0)
@@ -85,15 +85,15 @@ def tile_list_seabed_mosaic_scores_kernel(
             load_words(tile, words, a, slice(0, T))
             return tile
 
-        tab_w = [ring("tab_w", 2, [P, T], I32)]
-        load_words(tab_w[0], tab_words, 0, slice(0, T // 2))
+        idx1 = load_list("idx1", offs)
+        idx3 = load_list("idx3", offs3)
+        idx2 = load_list("idx2", offs2)
+        tab_w = [load_table("tab_w", tab_words, 0)]
         for q in range(QUADS):
             nc.sync.dma_start(
                 out=tab_sc[quad_rows(q, 4), :, :].bitcast(I32),
                 in_=tab_scales[:, 4 * q : 4 * q + 4, :].rearrange("a q t -> q a t").bitcast(I32),
             )
-        idx1 = load_list("idx1", offs)
-        load_words(tab_w[0], tab_words, 0, slice(T // 2, T))
         tab_w.append(load_table("tab_w", tab_words, 1))
         w1_w = ring("w1_w", 1, [P, 2, 2 * H], U8)
 
@@ -109,11 +109,9 @@ def tile_list_seabed_mosaic_scores_kernel(
                 out=w1_sc[quad_rows(q, 4), :, :].bitcast(I32),
                 in_=w1_scales[:, 4 * q : 4 * q + 4, :].rearrange("a q c -> q a c").bitcast(I32),
             )
-        idx3 = load_list("idx3", offs3)
         wg1_sb = keep("wg1_sb", [P, S], F32)
         nc.sync.dma_start(out=wg1_sb[:], in_=wg1)
         load_w1(W1_FIRST, SLICES)
-        idx2 = load_list("idx2", offs2)
 
         whole_list = [(slice(0, S), slice(0, S // 16))]
         list_halves = [(slice(c, c + S // 2), slice(c // 16, (c + S // 2) // 16)) for c in (0, S // 2)]
@@ -142,11 +140,11 @@ def tile_list_seabed_mosaic_scores_kernel(
                 nc.scalar.activation(tile[:, cols], acc[:], ACT.Tanh)
             h1.append(tile)
 
-        late_pages = [ring(tag, 1, [P, T2], F32) for tag in ("v_w", "w1_w", "w1_sc")]
+        late_pages = [ring(tag, 1, [P, T2], F32) for tag in ("v_w", "tab_sc", "w1_w", "w1_sc")]
         for page in late_pages:
             nc.gpsimd.memset(page[:].bitcast(I32), 0)
-        pa.append(late_pages[0])
-        pb = late_pages[1:]
+        pa.extend(late_pages[:2])
+        pb = late_pages[2:]
 
         def place_a(s):
             for cols, offsets in list_halves if s == 0 else whole_list:
@@ -156,6 +154,29 @@ def tile_list_seabed_mosaic_scores_kernel(
 
         for s in range(PA_PAGES):
             place_a(s)
+
+        w2_w = keep("w2_w", [P, 3, H], U32)
+        w2_sc = keep("w2_sc", [P, 3, H], U8)
+
+        def quantise_w2(a):
+            grouped = ring("wide_bf", 3, [P, H, PACK], BF16)
+            for h in range(2):
+                cols = slice(HALF * h, HALF * (h + 1))
+                tag, bufs = ("stage", 4) if a < 2 else ("tab_w", 2)
+                raw = ring(tag, bufs, [P, PACK, HALF], F32)
+                nc.sync.dma_start(
+                    out=raw[:], in_=w2[K_PASS * a : K_PASS * (a + 1), cols].rearrange("(p i) c -> p i c", i=PACK)
+                )
+                nc.scalar.copy(
+                    grouped[:, cols, :].rearrange("p (c n) i -> p c i n", n=4),
+                    raw[:].rearrange("p i (c n) -> p c i n", n=4),
+                )
+            nc.vector.quantize_mx(
+                out=w2_w[:, a, :].bitcast(FP8X4), scales=w2_sc[:, a, :], in_=grouped[:].rearrange("p c i -> p (c i)")
+            )
+
+        for a in range(3):
+            quantise_w2(a)
 
         for q in range(QUADS):
             nc.sync.dma_start(
@@ -174,34 +195,6 @@ def tile_list_seabed_mosaic_scores_kernel(
         nc.tensor.transpose(gz_ps[:], gz_rows[:], ident[:])
         gz_col = keep("gz_col", [P, SLICES], F32)
         nc.scalar.copy(gz_col[:], gz_ps[:, 0:SLICES])
-        idx4 = load_list("idx4", offs4)
-        wg2_sb = ring("wg2_w3", 1, [P, S], F32)
-        nc.sync.dma_start(out=wg2_sb[:], in_=wg2)
-
-        w2_w = keep("w2_w", [P, 3, H], U32)
-        w2_sc = keep("w2_sc", [P, 3, H], U8)
-
-        def load_w2(h, a):
-            raw = ring("stage", 4, [P, PACK, HALF], F32)
-            nc.sync.dma_start(
-                out=raw[:],
-                in_=w2[K_PASS * a : K_PASS * (a + 1), HALF * h : HALF * (h + 1)].rearrange("(p i) c -> p i c", i=PACK),
-            )
-            return raw
-
-        def quantise_w2(h, a, raw):
-            cols = slice(HALF * h, HALF * (h + 1))
-            grouped = ring("w2_bf", 3, [P, HALF, PACK], BF16)
-            nc.scalar.copy(
-                grouped[:].rearrange("p (c n) i -> p c i n", n=4),
-                raw[:].rearrange("p i (c n) -> p c i n", n=4),
-            )
-            nc.vector.quantize_mx(
-                out=w2_w[:, a, cols].bitcast(FP8X4),
-                scales=w2_sc[:, a, cols],
-                in_=grouped[:].rearrange("p c i -> p (c i)"),
-            )
-
         def load_chart(tag, bufs, pair):
             tile = ring(tag, bufs, [P, 2, T2], F32)
             nc.sync.dma_start(
@@ -209,11 +202,12 @@ def tile_list_seabed_mosaic_scores_kernel(
             )
             return tile
 
-        for h in range(2):
-            for a in range(3):
-                quantise_w2(h, a, load_w2(h, a))
-        chart_sb = [load_chart("tab_w", 2, 0), load_chart("tab_w", 2, 1)]
-        chart_sb.extend([load_chart("tab2_w", 3, 2), load_chart("tab2_w", 3, 3)])
+        chart_sb = [load_chart("stage", 4, 0), load_chart("stage", 4, 1)]
+        idx4 = load_list("idx4", offs4)
+        wg2_sb = ring("wg2_w3", 1, [P, S], F32)
+        nc.sync.dma_start(out=wg2_sb[:], in_=wg2)
+
+        chart_sb.extend([load_chart("tab_w", 2, 2), load_chart("tab_w", 2, 3)])
 
         w3_raw = keep("w3_raw", [P, GROUPS, N], I32)
         nc.sync.dma_start(out=w3_raw[:], in_=w3_words.rearrange("a p c i -> p a (c i)").bitcast(I32))
@@ -298,7 +292,8 @@ def tile_list_seabed_mosaic_scores_kernel(
 
         z_w = {}
         z_sc = keep("z_sc", [P, GROUPS, T2], U8)
-        z_bf = {}
+        z_bf0 = ring("wide_bf", 3, [P, T2, PACK], BF16)
+        z_bf1 = {}
 
         def group_z(g, c):
             h, b0 = divmod(CH * c // P, 4)
@@ -307,19 +302,22 @@ def tile_list_seabed_mosaic_scores_kernel(
             for b in range(2):
                 for u in range(2):
                     nc.tensor.transpose(turned[:, b, u, :], words[:, b0 + b, u, :], ident[:])
-            z_bf[g, c] = ring("z_bf", 6, [P, CH, PACK], BF16)
+            if g == 0:
+                grouped = z_bf0[:, CH * c : CH * (c + 1), :]
+            else:
+                z_bf1[c] = ring("z_bf1", 4, [P, CH, PACK], BF16)
+                grouped = z_bf1[c][:]
             move = nc.scalar.copy if g == 0 else nc.vector.tensor_copy
             move(
-                z_bf[g, c][:].bitcast(F32).rearrange("p (b j) u -> p b j u", b=2),
+                grouped.bitcast(F32).rearrange("p (b j) u -> p b j u", b=2),
                 turned[:].rearrange("p b u j -> p b j u"),
             )
 
-        def quantise_z(g, c):
-            cols = slice(CH * c, CH * (c + 1))
+        def quantise_z(g, cols, grouped):
             nc.vector.quantize_mx(
                 out=z_w[g][:, cols].bitcast(FP8X4),
                 scales=z_sc[:, g, cols],
-                in_=z_bf[g, c][:].rearrange("p j i -> p (j i)"),
+                in_=grouped[:].rearrange("p j i -> p (j i)"),
             )
 
         y_w = keep("y_w", [P, T2], U32)
@@ -380,12 +378,11 @@ def tile_list_seabed_mosaic_scores_kernel(
         w3_w = deal_w3()
         z_w[0] = ring("last", 1, [P, T2], U32)
         z_w[1] = keep("z_w1", [P, T2], U32)
-        for c in range(chunks):
-            quantise_z(0, c)
+        quantise_z(0, slice(0, T2), z_bf0)
         for c in range(chunks + 1):
             if c < chunks:
                 group_z(1, c)
-                quantise_z(1, c)
+                quantise_z(1, slice(CH * c, CH * (c + 1)), z_bf1[c])
             if c > 0:
                 score(c - 1)
         for q in range(QUADS):

@@ -80,21 +80,21 @@ def tile_list_seabed_mosaic_scores_kernel(
         def load_words(tile, words, a, cols):
             nc.sync.dma_start(out=tile[:, cols], in_=words[a].rearrange("p t i -> p (t i)").bitcast(I32)[:, cols])
 
-        def load_table(tag, words, a):
-            tile = ring(tag, words.shape[0], [P, T], I32)
+        def load_table(tag, bufs, words, a):
+            tile = ring(tag, bufs, [P, T], I32)
             load_words(tile, words, a, slice(0, T))
             return tile
 
         idx1 = load_list("idx1", offs)
         idx3 = load_list("idx3", offs3)
         idx2 = load_list("idx2", offs2)
-        tab_w = [load_table("tab_w", tab_words, 0)]
+        tab_w = [load_table("tab_w", 2, tab_words, 0)]
         for q in range(QUADS):
             nc.sync.dma_start(
                 out=tab_sc[quad_rows(q, 4), :, :].bitcast(I32),
                 in_=tab_scales[:, 4 * q : 4 * q + 4, :].rearrange("a q t -> q a t").bitcast(I32),
             )
-        tab_w.append(load_table("tab_w", tab_words, 1))
+        tab_w.append(load_table("tab_w", 2, tab_words, 1))
         w1_w = ring("w1_w", 1, [P, 2, 2 * H], U8)
 
         def load_w1(first, last):
@@ -178,12 +178,21 @@ def tile_list_seabed_mosaic_scores_kernel(
         for a in range(3):
             quantise_w2(a)
 
+        def load_chart(tag, bufs, pair):
+            tile = ring(tag, bufs, [P, 2, T2], F32)
+            nc.sync.dma_start(
+                out=tile[:], in_=chart[2 * P * pair : 2 * P * (pair + 1), :].rearrange("(s p) j -> p s j", p=P)
+            )
+            return tile
+
+        chart_sb = [load_chart("stage", 4, 0)]
+
         for q in range(QUADS):
             nc.sync.dma_start(
                 out=tab2_sc[quad_rows(q, 12), :].bitcast(I32),
                 in_=tab2_scales[:, 4 * q : 4 * q + 4, :].bitcast(I32),
             )
-        tab2_w = [load_table("tab2_w", tab2_words, a) for a in range(3)]
+        tab2_w = [load_table("tab2_w%d" % a, 1, tab2_words, a) for a in range(3)]
         v2_sc = keep("v2_sc", [P, S], U8)
         v2_w = keep("v2_w", [P, 3, S], U32)
         nc.vector.tensor_copy(v2_sc[:], tab2_sc[:].indirect(idx2[:]))
@@ -195,14 +204,7 @@ def tile_list_seabed_mosaic_scores_kernel(
         nc.tensor.transpose(gz_ps[:], gz_rows[:], ident[:])
         gz_col = keep("gz_col", [P, SLICES], F32)
         nc.scalar.copy(gz_col[:], gz_ps[:, 0:SLICES])
-        def load_chart(tag, bufs, pair):
-            tile = ring(tag, bufs, [P, 2, T2], F32)
-            nc.sync.dma_start(
-                out=tile[:], in_=chart[2 * P * pair : 2 * P * (pair + 1), :].rearrange("(s p) j -> p s j", p=P)
-            )
-            return tile
-
-        chart_sb = [load_chart("stage", 4, 0), load_chart("stage", 4, 1)]
+        chart_sb.append(load_chart("stage", 4, 1))
         idx4 = load_list("idx4", offs4)
         wg2_sb = ring("wg2_w3", 1, [P, S], F32)
         nc.sync.dma_start(out=wg2_sb[:], in_=wg2)
@@ -216,7 +218,6 @@ def tile_list_seabed_mosaic_scores_kernel(
                 out=w3_sc[quad_rows(q, 8), :].bitcast(I32),
                 in_=w3_scales[:, 4 * q : 4 * q + 4, :].bitcast(I32),
             )
-        w3_sd = keep("w3_sd", [P, PACK, P], U8)
 
         def deal_w3():
             w3_w = ring("wg2_w3", 1, [P, GROUPS, PACK, P], I32)
@@ -224,8 +225,9 @@ def tile_list_seabed_mosaic_scores_kernel(
                 w3_w[:].rearrange("p a t (q n) -> p a q t n", n=4),
                 w3_raw[:].rearrange("p a (q n t) -> p a q t n", n=4, t=PACK),
             )
+            w3_sd = ring("w3_raw", 1, [P, PACK, P], U8)
             nc.vector.tensor_copy(w3_sd[:], w3_sc[:].rearrange("p (q t) -> p t q", t=PACK))
-            return w3_w
+            return w3_w, w3_sd
 
         def reduce_d(s):
             acc = bank("mm", 3, [P, S])
@@ -257,8 +259,9 @@ def tile_list_seabed_mosaic_scores_kernel(
             nc.scalar.activation(phase[s][:], phase[s][:], ACT.Sin, scale=2.0 * math.pi)
 
         def take_max(s):
-            upper[s] = chart_sb[s // 2][:, s % 2, :]
-            nc.vector.tensor_tensor(upper[s], pa[s % PA_PAGES][:], upper[s], ALU.max)
+            rows = chart_sb[s // 2][:, s % 2, :]
+            upper[s] = ring("tab2_w2", 1, [P, T2], F32)[:] if s == 0 else rows
+            nc.vector.tensor_tensor(upper[s], pa[s % PA_PAGES][:], rows, ALU.max)
             if s + PA_PAGES < SLICES:
                 place_a(s + PA_PAGES)
 
@@ -375,7 +378,7 @@ def tile_list_seabed_mosaic_scores_kernel(
                 gain_max(s + LEAD)
             if 4 <= s < 4 + chunks:
                 group_z(0, s - 4)
-        w3_w = deal_w3()
+        w3_w, w3_sd = deal_w3()
         z_w[0] = ring("last", 1, [P, T2], U32)
         z_w[1] = keep("z_w1", [P, T2], U32)
         quantise_z(0, slice(0, T2), z_bf0)

@@ -64,13 +64,12 @@ def tile_list_seabed_mosaic_scores_kernel(
         nc.gpsimd.memset(tab_sc[:, 1, :].bitcast(I32), 0)
         nc.vector.memset(w1_sc[:].bitcast(I32), 0)
         nc.vector.memset(tab2_sc[:].bitcast(I32), 0)
-        pa = [keep("pa%d" % i, [P, T2], F32) for i in range(PA_PAGES - 2)]
+        pa = [keep("pa%d" % i, [P, T2], F32) for i in range(PA_PAGES)]
+        pb = [keep("pb%d" % i, [P, T2], F32) for i in range(PB_PAGES)]
         ident = keep("ident", [P, P], F32)
-        for page in pa:
-            nc.vector.memset(page[:].bitcast(I32), 0)
-        nc.gpsimd.memset(gz_rows[:], 0.0)
+        nc.vector.memset(gz_rows[:], 0.0)
         make_identity(nc, ident[:])
-        nc.gpsimd.memset(w3_sc[:].bitcast(I32), 0)
+        nc.vector.memset(w3_sc[:].bitcast(I32), 0)
 
         def load_list(name, src):
             tile = lists.tile([P, S // 16], U16, name=name, tag=name)
@@ -123,6 +122,9 @@ def tile_list_seabed_mosaic_scores_kernel(
         for cols, offsets in list_halves:
             nc.vector.tensor_copy(v_w[:, 1, cols], tab_w[1][:].bitcast(U32).indirect(idx1[:, offsets]))
 
+        for page in pa + pb:
+            nc.vector.memset(page[:].bitcast(I32), 0)
+
         h1 = []
         for s in range(SLICES):
             tile = ring("h1", SLICES, [P, S], F32)
@@ -139,12 +141,6 @@ def tile_list_seabed_mosaic_scores_kernel(
                     )
                 nc.scalar.activation(tile[:, cols], acc[:], ACT.Tanh)
             h1.append(tile)
-
-        late_pages = [ring(tag, 1, [P, T2], F32) for tag in ("v_w", "tab_sc", "w1_w", "w1_sc")]
-        for page in late_pages:
-            nc.gpsimd.memset(page[:].bitcast(I32), 0)
-        pa.extend(late_pages[:2])
-        pb = late_pages[2:]
 
         def place_a(s):
             for cols, offsets in list_halves if s == 0 else whole_list:
@@ -279,7 +275,8 @@ def tile_list_seabed_mosaic_scores_kernel(
             g, sl = divmod(s, SL_PER_GROUP)
             for h in range(T2 // HALF):
                 if sl == 0:
-                    z_t[g, h] = ring("z_t", 4, [P, 4, 2, P, 2], BF16)
+                    tag, bufs = ("tab2_w%d" % h, 1) if g == 0 else ("z_t", 2)
+                    z_t[g, h] = ring(tag, bufs, [P, 4, 2, P, 2], BF16)
                 tsum = bank("tsum", 3, [P, 4, P])
                 for term, src in enumerate((upper[s], pb[s % PB_PAGES])):
                     for b in range(4):

import math
from contextlib import ExitStack

import concourse.mybir as mybir
from concourse.masks import make_identity

K, K2, T, S, H, N, T2 = 1024, 1536, 2048, 512, 1024, 512, 1024
FLOPS = 2 * (K * H * S + K2 * H * S + H * N * T2)

F32 = mybir.dt.float32
BF16 = mybir.dt.bfloat16
I32 = mybir.dt.int32
U32 = mybir.dt.uint32
U16 = mybir.dt.uint16
U8 = mybir.dt.uint8
FP8X4 = mybir.dt.float8_e4m3fn_x4
FP4X4 = mybir.dt.float4_e2m1fn_x4
ACT = mybir.ActivationFunctionType
ALU = mybir.AluOpType

P = 128
PACK = 4
K_PASS = P * PACK
SLICES = H // P
GROUPS = H // K_PASS
SL_PER_GROUP = K_PASS // P
QUADS = 4
PA_PAGES = 5
PB_PAGES = 2
HALF = 512
CH = 256
W1_FIRST = 2
LEAD = 4


def tile_list_seabed_mosaic_scores_kernel(
    tc, tab_words, tab_scales, tab2_words, tab2_scales, offs, offs2, offs3, offs4,
    w1_words, w1_scales, w2, w3_words, w3_scales, wg1, wg2, chart, gz, out_0, out_1, out_2,
):
    nc = tc.nc
    with ExitStack() as ctx:
        lists = ctx.enter_context(tc.tile_pool(name="lists", bufs=1))
        sb = ctx.enter_context(tc.tile_pool(name="sb", bufs=1))
        ps = ctx.enter_context(tc.psum_pool(name="ps", bufs=1))

        def keep(name, shape, dtype):
            return sb.tile(shape, dtype, name=name, tag=name, bufs=1, align_bytes=64)

        def ring(tag, bufs, shape, dtype):
            return sb.tile(shape, dtype, name=tag, tag=tag, bufs=bufs, align_bytes=64)

        def bank(tag, bufs, shape):
            return ps.tile(shape, F32, name=tag, tag=tag, bufs=bufs)

        def quad_rows(q, rows):
            return slice(32 * q, 32 * q + rows)

        tab_sc = keep("tab_sc", [P, 2, T], U8)
        w1_sc = keep("w1_sc", [P, 2, H], U8)
        tab2_sc = keep("tab2_sc", [P, T], U8)
        w3_sc = keep("w3_sc", [P, N], U8)
        gz_rows = keep("gz_rows", [P, P], F32)
        nc.vector.memset(tab_sc[:, 0, :].bitcast(I32), 0)
        nc.gpsimd.memset(tab_sc[:, 1, :].bitcast(I32), 0)
        nc.vector.memset(w1_sc[:].bitcast(I32), 0)
        nc.vector.memset(tab2_sc[:].bitcast(I32), 0)
        pa = [keep("pa%d" % i, [P, T2], F32) for i in range(PA_PAGES)]
        pb = [keep("pb%d" % i, [P, T2], F32) for i in range(PB_PAGES)]
        ident = keep("ident", [P, P], F32)
        nc.vector.memset(gz_rows[:], 0.0)
        make_identity(nc, ident[:])
        nc.vector.memset(w3_sc[:].bitcast(I32), 0)

        def load_list(name, src):
            tile = lists.tile([P, S // 16], U16, name=name, tag=name)
            nc.sync.dma_start(tile[:], src)
            return tile

        def load_words(tile, words, a, cols):
            nc.sync.dma_start(out=tile[:, cols], in_=words[a].rearrange("p t i -> p (t i)").bitcast(I32)[:, cols])

        def load_table(tag, bufs, words, a):
            tile = ring(tag, bufs, [P, T], I32)
            load_words(tile, words, a, slice(0, T))
            return tile

        idx1 = load_list("idx1", offs)
        idx3 = load_list("idx3", offs3)
        idx2 = load_list("idx2", offs2)
        tab_w = [load_table("tab_w", 2, tab_words, 0)]
        for q in range(QUADS):
            nc.sync.dma_start(
                out=tab_sc[quad_rows(q, 4), :, :].bitcast(I32),
                in_=tab_scales[:, 4 * q : 4 * q + 4, :].rearrange("a q t -> q a t").bitcast(I32),
            )
        tab_w.append(load_table("tab_w", 2, tab_words, 1))
        w1_w = ring("w1_w", 1, [P, 2, 2 * H], U8)

        def load_w1(first, last):
            cols = slice(2 * P * first, 2 * P * last)
            nc.sync.dma_start(
                out=w1_w[:, :, cols].bitcast(I32), in_=w1_words[:, :, cols].rearrange("a p c -> p a c").bitcast(I32)
            )

        load_w1(0, W1_FIRST)
        for q in range(QUADS):
            nc.sync.dma_start(
                out=w1_sc[quad_rows(q, 4), :, :].bitcast(I32),
                in_=w1_scales[:, 4 * q : 4 * q + 4, :].rearrange("a q c -> q a c").bitcast(I32),
            )
        wg1_sb = keep("wg1_sb", [P, S], F32)
        nc.sync.dma_start(out=wg1_sb[:], in_=wg1)
        load_w1(W1_FIRST, SLICES)

        whole_list = [(slice(0, S), slice(0, S // 16))]
        list_halves = [(slice(c, c + S // 2), slice(c // 16, (c + S // 2) // 16)) for c in (0, S // 2)]
        v_sc = keep("v_sc", [P, 2, S], U8)
        v_w = keep("v_w", [P, 2, S], U32)
        for a in range(2):
            nc.vector.tensor_copy(v_sc[:, a, :], tab_sc[:, a, :].indirect(idx1[:]))
        nc.vector.tensor_copy(v_w[:, 0, :], tab_w[0][:].bitcast(U32).indirect(idx1[:]))
        for cols, offsets in list_halves:
            nc.vector.tensor_copy(v_w[:, 1, cols], tab_w[1][:].bitcast(U32).indirect(idx1[:, offsets]))

        for page in pa + pb:
            nc.vector.memset(page[:].bitcast(I32), 0)

        h1 = []
        for s in range(SLICES):
            tile = ring("h1", SLICES, [P, S], F32)
            for cols, offsets in list_halves if s == 0 else whole_list:
                acc = bank("mm", 3, [P, cols.stop - cols.start])
                for a in range(2):
                    nc.tensor.matmul_mx(
                        out=acc[:],
                        lhsT=w1_w[:, a, 2 * P * s : 2 * P * (s + 1)].bitcast(FP4X4),
                        lhsT_scale=w1_sc[:, a, P * s : P * (s + 1)],
                        rhs=v_w[:, a, cols].bitcast(FP8X4),
                        rhs_scale=v_sc[:, a, cols],
                        start=(a == 0), stop=(a == 1),
                    )
                nc.scalar.activation(tile[:, cols], acc[:], ACT.Tanh)
            h1.append(tile)

        def place_a(s):
            for cols, offsets in list_halves if s == 0 else whole_list:
                nc.vector.tensor_tensor(
                    pa[s % PA_PAGES][:].indirect(idx3[:, offsets]), h1[s][:, cols], wg1_sb[:, cols], ALU.mult
                )

        for s in range(PA_PAGES):
            place_a(s)

        w2_w = keep("w2_w", [P, 3, H], U32)
        w2_sc = keep("w2_sc", [P, 3, H], U8)

        def quantise_w2(a):
            grouped = ring("wide_bf", 3, [P, H, PACK], BF16)
            for h in range(2):
                cols = slice(HALF * h, HALF * (h + 1))
                tag, bufs = ("stage", 4) if a < 2 else ("tab_w", 2)
                raw = ring(tag, bufs, [P, PACK, HALF], F32)
                nc.sync.dma_start(
                    out=raw[:], in_=w2[K_PASS * a : K_PASS * (a + 1), cols].rearrange("(p i) c -> p i c", i=PACK)
                )
                nc.scalar.copy(
                    grouped[:, cols, :].rearrange("p (c n) i -> p c i n", n=4),
                    raw[:].rearrange("p i (c n) -> p c i n", n=4),
                )
            nc.vector.quantize_mx(
                out=w2_w[:, a, :].bitcast(FP8X4), scales=w2_sc[:, a, :], in_=grouped[:].rearrange("p c i -> p (c i)")
            )

        for a in range(3):
            quantise_w2(a)

        def load_chart(tag, bufs, pair):
            tile = ring(tag, bufs, [P, 2, T2], F32)
            nc.sync.dma_start(
                out=tile[:], in_=chart[2 * P * pair : 2 * P * (pair + 1), :].rearrange("(s p) j -> p s j", p=P)
            )
            return tile

        chart_sb = [load_chart("stage", 4, 0)]

        for q in range(QUADS):
            nc.sync.dma_start(
                out=tab2_sc[quad_rows(q, 12), :].bitcast(I32),
                in_=tab2_scales[:, 4 * q : 4 * q + 4, :].bitcast(I32),
            )
        tab2_w = [load_table("tab2_w%d" % a, 1, tab2_words, a) for a in range(3)]
        v2_sc = keep("v2_sc", [P, S], U8)
        v2_w = keep("v2_w", [P, 3, S], U32)
        nc.vector.tensor_copy(v2_sc[:], tab2_sc[:].indirect(idx2[:]))
        for a in range(3):
            nc.vector.tensor_copy(v2_w[:, a, :], tab2_w[a][:].bitcast(U32).indirect(idx2[:]))

        nc.sync.dma_start(out=gz_rows[0:SLICES, :], in_=gz.rearrange("(s p) -> s p", p=P))
        gz_ps = bank("tw", 2, [P, P])
        nc.tensor.transpose(gz_ps[:], gz_rows[:], ident[:])
        gz_col = keep("gz_col", [P, SLICES], F32)
        nc.scalar.copy(gz_col[:], gz_ps[:, 0:SLICES])
        chart_sb.append(load_chart("stage", 4, 1))
        idx4 = load_list("idx4", offs4)
        wg2_sb = ring("wg2_w3", 1, [P, S], F32)
        nc.sync.dma_start(out=wg2_sb[:], in_=wg2)

        chart_sb.extend([load_chart("tab_w", 2, 2), load_chart("tab_w", 2, 3)])

        w3_raw = keep("w3_raw", [P, GROUPS, N], I32)
        nc.sync.dma_start(out=w3_raw[:], in_=w3_words.rearrange("a p c i -> p a (c i)").bitcast(I32))
        for q in range(QUADS):
            nc.sync.dma_start(
                out=w3_sc[quad_rows(q, 8), :].bitcast(I32),
                in_=w3_scales[:, 4 * q : 4 * q + 4, :].bitcast(I32),
            )

        def deal_w3():
            w3_w = ring("wg2_w3", 1, [P, GROUPS, PACK, P], I32)
            nc.vector.tensor_copy(
                w3_w[:].rearrange("p a t (q n) -> p a q t n", n=4),
                w3_raw[:].rearrange("p a (q n t) -> p a q t n", n=4, t=PACK),
            )
            w3_sd = ring("w3_raw", 1, [P, PACK, P], U8)
            nc.vector.tensor_copy(w3_sd[:], w3_sc[:].rearrange("p (q t) -> p t q", t=PACK))
            return w3_w, w3_sd

        def reduce_d(s):
            acc = bank("mm", 3, [P, S])
            for a in range(3):
                nc.tensor.matmul_mx(
                    out=acc[:],
                    lhsT=w2_w[:, a, P * s : P * (s + 1)].bitcast(FP8X4),
                    lhsT_scale=w2_sc[:, a, P * s : P * (s + 1)],
                    rhs=v2_w[:, a, :].bitcast(FP8X4),
                    rhs_scale=v2_sc[4 * a : P, :],
                    start=(a == 0), stop=(a == 2),
                )
            turns = ring("turns", 4, [P, S], F32) if s < SLICES - 1 else ring("last", 1, [P, S], F32)
            nc.scalar.activation(turns[:], acc[:], ACT.Abs, scale=1.0 / (2.0 * math.pi))
            whole = ring("whole", 2, [P, S], U32)
            nc.scalar.activation(whole[:], turns[:], ACT.Relu, bias=-0.25)
            nc.vector.scalar_tensor_tensor(
                out=turns[:], in0=turns[:], scalar=0.25, in1=whole[:].bitcast(I32), op0=ALU.subtract, op1=ALU.subtract
            )
            return acc, turns

        z_t = {}

        d_acc = {}
        phase = {}
        upper = {}

        def cosine(s):
            nc.scalar.activation(phase[s][:], phase[s][:], ACT.Sin, scale=2.0 * math.pi)

        def take_max(s):
            rows = chart_sb[s // 2][:, s % 2, :]
            upper[s] = ring("tab2_w2", 1, [P, T2], F32)[:] if s == 0 else rows
            nc.vector.tensor_tensor(upper[s], pa[s % PA_PAGES][:], rows, ALU.max)
            if s + PA_PAGES < SLICES:
                place_a(s + PA_PAGES)

        def gain_max(s):
            nc.scalar.activation(upper[s], upper[s], ACT.Copy, scale=gz_col[:, s : s + 1])

        def place_b(s):
            nc.vector.scalar_tensor_tensor(
                out=phase[s][:], in0=d_acc[s][:], scalar=gz_col[:, s : s + 1], in1=phase[s][:],
                op0=ALU.mult, op1=ALU.mult,
            )
            nc.vector.tensor_tensor(pb[s % PB_PAGES][:].indirect(idx4[:]), phase[s][:], wg2_sb[:], ALU.mult)

        def turn_sum(s):
            g, sl = divmod(s, SL_PER_GROUP)
            for h in range(T2 // HALF):
                if sl == 0:
                    tag, bufs = ("tab2_w%d" % h, 1) if g == 0 else ("z_t", 2)
                    z_t[g, h] = ring(tag, bufs, [P, 4, 2, P, 2], BF16)
                tsum = bank("tsum", 3, [P, 4, P])
                for term, src in enumerate((upper[s], pb[s % PB_PAGES])):
                    for b in range(4):
                        cols = slice(HALF * h + P * b, HALF * h + P * (b + 1))
                        nc.tensor.matmul(
                            tsum[:, b, :], src[:, cols], ident[:],
                            start=(term == 0 and b == 0), stop=(term == 1 and b == 3), is_transpose=True,
                        )
                nc.scalar.copy(
                    z_t[g, h][:, :, :, 32 * sl : 32 * (sl + 1), :],
                    tsum[:].rearrange("j b (q u e) -> j b u q e", u=2, e=2),
                )

        z_w = {}
        z_sc = keep("z_sc", [P, GROUPS, T2], U8)
        z_bf0 = ring("wide_bf", 3, [P, T2, PACK], BF16)
        z_bf1 = {}

        def group_z(g, c):
            h, b0 = divmod(CH * c // P, 4)
            words = z_t[g, h][:].rearrange("j b u p e -> j b u (p e)").bitcast(F32)
            turned = bank("tw", 2, [P, 2, 2, P])
            for b in range(2):
                for u in range(2):
                    nc.tensor.transpose(turned[:, b, u, :], words[:, b0 + b, u, :], ident[:])
            if g == 0:
                grouped = z_bf0[:, CH * c : CH * (c + 1), :]
            else:
                z_bf1[c] = ring("z_bf1", 4, [P, CH, PACK], BF16)
                grouped = z_bf1[c][:]
            move = nc.scalar.copy if g == 0 else nc.vector.tensor_copy
            move(
                grouped.bitcast(F32).rearrange("p (b j) u -> p b j u", b=2),
                turned[:].rearrange("p b u j -> p b j u"),
            )

        def quantise_z(g, cols, grouped):
            nc.vector.quantize_mx(
                out=z_w[g][:, cols].bitcast(FP8X4),
                scales=z_sc[:, g, cols],
                in_=grouped[:].rearrange("p j i -> p (j i)"),
            )

        y_w = keep("y_w", [P, T2], U32)
        y_sc = keep("y_sc", [P, T2], U8)
        y_rows = out_0.rearrange("(p t) j -> p t j", t=PACK)
        y_words = out_1[0].rearrange("p m t -> p (m t)").bitcast(I32)

        def score(c):
            cols = slice(CH * c, CH * (c + 1))
            y = ring("stage", 4, [P, PACK, CH], F32)
            for pair in range(2):
                acc = bank("mm", 3, [P, 2, CH])
                for i in range(2):
                    t = 2 * pair + i
                    for g in range(GROUPS):
                        nc.tensor.matmul_mx(
                            out=acc[:, i, :],
                            lhsT=w3_w[:, g, t, :].bitcast(FP8X4),
                            lhsT_scale=w3_sd[4 * g : P, t, :],
                            rhs=z_w[g][:, cols].bitcast(FP8X4),
                            rhs_scale=z_sc[:, g, cols],
                            start=(g == 0), stop=(g == GROUPS - 1),
                        )
                nc.scalar.activation(y[:, 2 * pair : 2 * pair + 2, :], acc[:], ACT.Gelu_apprx_tanh)
            nc.sync.dma_start(out=y_rows[:, :, cols], in_=y[:])
            grouped = ring("y_bf", 2, [P, CH, PACK], BF16)
            nc.vector.tensor_copy(
                grouped[:].rearrange("p (c n) t -> p c t n", n=4),
                y[:].rearrange("p t (c n) -> p c t n", n=4),
            )
            nc.vector.quantize_mx(
                out=y_w[:, cols].bitcast(FP8X4),
                scales=y_sc[:, cols],
                in_=grouped[:].rearrange("p j t -> p (j t)"),
            )
            nc.sync.dma_start(out=y_words[:, cols], in_=y_w[:, cols].bitcast(I32))

        chunks = T2 // CH
        for s in range(LEAD):
            take_max(s)
            gain_max(s)
        for s in range(2):
            d_acc[s], phase[s] = reduce_d(s)
        cosine(0)
        for s in range(SLICES):
            place_b(s)
            if s + 2 < SLICES:
                d_acc[s + 2], phase[s + 2] = reduce_d(s + 2)
            if s + 1 < SLICES:
                cosine(s + 1)
            if s + LEAD < SLICES:
                take_max(s + LEAD)
            turn_sum(s)
            if s + LEAD < SLICES:
                gain_max(s + LEAD)
            if 4 <= s < 4 + chunks:
                group_z(0, s - 4)
        w3_w, w3_sd = deal_w3()
        z_w[0] = ring("last", 1, [P, T2], U32)
        z_w[1] = keep("z_w1", [P, T2], U32)
        quantise_z(0, slice(0, T2), z_bf0)
        for c in range(chunks + 1):
            if c < chunks:
                group_z(1, c)
                quantise_z(1, slice(CH * c, CH * (c + 1)), z_bf1[c])
            if c > 0:
                score(c - 1)
        for q in range(QUADS):
            nc.sync.dma_start(
                out=out_2[0, 4 * q : 4 * q + 4, :].bitcast(I32), in_=y_sc[quad_rows(q, 4), :].bitcast(I32)
            )
